import numpy as np
import ml_dtypes


def mxq(x, axis, fmt="e4m3"):
    dtype, down = {"e4m3": (ml_dtypes.float8_e4m3fn, 7), "e5m2": (ml_dtypes.float8_e5m2, 14)}[fmt]
    v = np.moveaxis(np.asarray(x, np.float32).astype(ml_dtypes.bfloat16).astype(np.float64), axis, -1)
    blocks = v.reshape(v.shape[:-1] + (-1, 32))
    amax = np.abs(blocks).max(-1, keepdims=True)
    byte = np.maximum(np.where(amax > 0, np.frexp(amax)[1] - 1 + 127, 0) - down, 1)
    scale = np.exp2(byte - 127.0)
    codes = (blocks / scale).astype(np.float32).astype(dtype).astype(np.float64)
    return np.moveaxis((codes * scale).reshape(v.shape), -1, axis)


WIDE = False


def mx_kscale(k):
    if not WIDE:
        return np.ones(k)
    levels = np.array([30, -30])
    if k % 512:
        return np.exp2(np.random.permutation(np.resize(levels, k // 32))).repeat(32)
    a = np.empty((k // 512, 16))
    for p in range(k // 512):
        a[p, :8] = np.random.permutation(np.resize(levels, 8))
        for g in range(8):
            far = levels[np.abs(levels - a[p, g]) >= 10]
            a[p, g + 8] = far[np.random.randint(len(far))]
    return np.exp2(a.ravel()).repeat(32)


def f64(x):
    return np.asarray(x).astype(np.float64)


def striped(idx):
    return np.tile(np.asarray(idx).reshape(-1, 16).T, (8, 1)).astype(np.uint16)


def unstriped(offs):
    return offs[:16].T.reshape(-1).astype(np.int64)


E2M1 = np.array([0.0, 0.5, 1.0, 1.5, 2.0, 3.0, 4.0, 6.0, -0.0, -0.5, -1.0, -1.5, -2.0, -3.0, -4.0, -6.0])


def pack_weight(w, fmt):
    k, n = w.shape
    w = f64(np.asarray(w, np.float32).astype(ml_dtypes.bfloat16)).reshape(k // 32, 32, n)
    amax = np.abs(w).max(1)
    if fmt in ("e4m3", "e5m2"):
        byte = np.frexp(amax)[1] - 1 + 127 - (7 if fmt == "e4m3" else 14)
    else:
        mant, ex = np.frexp(amax / 6.0)
        byte = np.where(mant > 0.5, ex, ex - 1) + 127
    byte = np.clip(np.where(amax > 0, byte, 1), 1, 254)
    scaled = (w * np.exp2(127.0 - byte)[:, None, :]).reshape(k, n).astype(np.float32)
    by_word = np.ascontiguousarray(scaled.reshape(k // 512, 128, 4, n).transpose(0, 1, 3, 2))
    if fmt in ("e4m3", "e5m2"):
        words = by_word.astype(ml_dtypes.float8_e4m3fn if fmt == "e4m3" else ml_dtypes.float8_e5m2).view(np.uint8)
    else:
        c = by_word.astype(ml_dtypes.float4_e2m1fn).view(np.uint8) & 0xF
        words = (c[..., 0::2] | (c[..., 1::2] << 4)).reshape(k // 512, 128, 2 * n)
    return np.ascontiguousarray(words), np.ascontiguousarray(byte.astype(np.uint8).reshape(k // 512, 16, n))


def unpack_weight(words, scales, fmt):
    g, _, n = scales.shape
    words = np.ascontiguousarray(words).reshape(g, 128, n, -1)
    if fmt in ("e4m3", "e5m2"):
        vals = words.view(ml_dtypes.float8_e4m3fn if fmt == "e4m3" else ml_dtypes.float8_e5m2).astype(np.float64)
    else:
        nib = np.empty((g, 128, n, 4), np.uint8)
        nib[..., 0::2] = words & 0xF
        nib[..., 1::2] = words >> 4
        vals = E2M1[nib]
    vals = vals * np.repeat(np.exp2(scales.astype(np.float64) - 127.0), 8, axis=1)[..., None]
    return vals.transpose(0, 1, 3, 2).reshape(g * 512, n)


def sigmoid(v):
    return 1.0 / (1.0 + np.exp(-v))


def sgn(shape):
    return np.random.uniform(0.5, 2.0, shape) * np.where(np.random.standard_normal(shape) < 0, -1.0, 1.0)


K, T, J, R, F, Z, O, N, E = 512, 1024, 256, 512, 512, 1024, 128, 256, 1024


def setup_inputs():
    n = np.random.standard_normal
    idx = np.random.permutation(T)[:J]
    idx2 = np.random.permutation(Z)[:J]
    idx3 = np.random.permutation(J)[:O]
    idx4 = np.random.permutation(J)[:O]
    idx5 = np.random.permutation(J)[:O]
    idx6 = np.random.permutation(T)[:O]
    idx7 = np.random.permutation(E)[:O]
    fk = mx_kscale(K)
    ff = mx_kscale(F)
    fr = mx_kscale(R)
    xtp = pack_weight(n((K, T)) / fk[:, None], "e4m3")
    xop = pack_weight(n((F, Z)) / ff[:, None], "e2m1")
    wp = pack_weight(n((K, R)) * 1 / np.sqrt(K) * fk[:, None], "e2m1")
    w2p = pack_weight(n((F, R)) * 1 / np.sqrt(F) * ff[:, None], "e5m2")
    wbp = pack_weight(n((R, N)) * 1 / np.sqrt(R) / fr[:, None], "e5m2")
    wsp = pack_weight(n((K, N)) * 1 / np.sqrt(K) * fk[:, None], "e5m2")
    return {
        "xt_words": xtp[0],
        "xt_scales": xtp[1],
        "xo_words": xop[0],
        "xo_scales": xop[1],
        "w_words": wp[0],
        "w_scales": wp[1],
        "w2_words": w2p[0],
        "w2_scales": w2p[1],
        "sa": (np.random.uniform(0.5, 1.6, (R, 1)) * fr[:, None]).astype(np.float32),
        "sb": (np.random.uniform(0.5, 1.6, (R, 1)) * fr[:, None]).astype(np.float32),
        "sg": (sgn((R, 1))).astype(np.float32),
        "wb_words": wbp[0],
        "wb_scales": wbp[1],
        "ws_words": wsp[0],
        "ws_scales": wsp[1],
        "offs": striped(idx),
        "offs2": striped(idx2),
        "offs3": striped(idx3),
        "offs4": striped(idx4),
        "offs5": striped(idx5),
        "offs6": striped(idx6),
        "offs7": striped(idx7),
    }


def reference(xt_words, xt_scales, xo_words, xo_scales, w_words, w_scales, w2_words, w2_scales, sa, sb, sg, wb_words, wb_scales, ws_words, ws_scales, offs, offs2, offs3, offs4, offs5, offs6, offs7):
    idx = unstriped(offs)
    idx2 = unstriped(offs2)
    idx3 = unstriped(offs3)
    idx4 = unstriped(offs4)
    idx5 = unstriped(offs5)
    idx6 = unstriped(offs6)
    idx7 = unstriped(offs7)
    xtu = unpack_weight(xt_words, xt_scales, "e4m3")
    xou = unpack_weight(xo_words, xo_scales, "e2m1")
    wu = unpack_weight(w_words, w_scales, "e2m1")
    w2u = unpack_weight(w2_words, w2_scales, "e5m2")
    wbu = unpack_weight(wb_words, wb_scales, "e5m2")
    wsu = unpack_weight(ws_words, ws_scales, "e5m2")
    xtidxg = xtu[:, idx]
    a = wu.T @ xtidxg
    xoidx2g = xou[:, idx2]
    b = w2u.T @ xoidx2g
    lb = b[:, 0:1]
    hid = a[:, idx3] * f64(sa) * sigmoid(a[:, idx4] * f64(sg) + lb) - b[:, idx5] * f64(sb)
    hidq = mxq(hid, 0, "e4m3")
    xtidx6g = xtu[:, idx6]
    p = wbu.T @ hidq + wsu.T @ xtidx6g
    y = np.zeros((N, E))
    y[:, idx7] = p
    return y

@@ -1,0 +1,201 @@
+from contextlib import ExitStack
+
+import concourse.mybir as mybir
+
+K, T, J, R, F, Z, O, N, E = 512, 1024, 256, 512, 512, 1024, 128, 256, 1024
+FLOPS = 2 * K * R * J + 2 * F * R * J + 2 * R * N * O + 2 * K * N * O
+
+P = 128
+PACK = 4
+QUADS = 4
+ROWS = 4
+
+F32 = mybir.dt.float32
+BF16 = mybir.dt.bfloat16
+I32 = mybir.dt.int32
+U32 = mybir.dt.uint32
+U16 = mybir.dt.uint16
+U8 = mybir.dt.uint8
+E4M3 = mybir.dt.float8_e4m3fn_x4
+E5M2 = mybir.dt.float8_e5m2_x4
+E2M1 = mybir.dt.float4_e2m1fn_x4
+ACT = mybir.ActivationFunctionType
+ALU = mybir.AluOpType
+
+
+def tile_list_offsetlead_twotab_further_scattered_kernel(
+    tc, xt_words, xt_scales, xo_words, xo_scales, w_words, w_scales, w2_words, w2_scales, sa, sb, sg,
+    wb_words, wb_scales, ws_words, ws_scales, offs, offs2, offs3, offs4, offs5, offs6, offs7, out,
+):
+    nc = tc.nc
+    with ExitStack() as ctx:
+        lists = ctx.enter_context(tc.tile_pool(name="lists", bufs=1))
+        keep = ctx.enter_context(tc.tile_pool(name="keep", bufs=1))
+        psum = ctx.enter_context(tc.psum_pool(name="psum", bufs=1))
+
+        def tile(name, shape, dtype):
+            return keep.tile(shape, dtype, name=name, align_bytes=64)
+
+        def load_list(name, src):
+            dst = lists.tile(list(src.shape), U16, name=name)
+            nc.sync.dma_start(dst[:], src)
+            return dst
+
+        def load_words(name, src, columns, dtype, queue):
+            dst = tile(name, [P, columns], dtype)
+            rows = src[0] if src.ndim == 3 else src[0].rearrange("p c t -> p (c t)")
+            queue.dma_start(dst[:].bitcast(I32), rows.bitcast(I32))
+            return dst
+
+        def zeroed_plane(name, columns):
+            dst = tile(name, [P, columns], U8)
+            nc.vector.memset(dst[:].bitcast(I32), 0)
+            return dst
+
+        def load_plane(plane, src, queue):
+            for q in range(QUADS):
+                queue.dma_start(plane[32 * q : 32 * q + ROWS, :].bitcast(I32), src[0, ROWS * q : ROWS * (q + 1), :].bitcast(I32))
+
+        def load_staged(name, src, columns, queue):
+            dst = tile(name, [ROWS, QUADS, columns // 4], I32)
+            queue.dma_start(dst[:], src[0].bitcast(I32).rearrange("(q r) c -> r q c", r=ROWS))
+            return dst
+
+        def spread(plane, staged):
+            for q in range(QUADS):
+                nc.vector.tensor_copy(plane[32 * q : 32 * q + ROWS, :].bitcast(I32), staged[:, q, :])
+
+        def deal(copy, name, src, dtype):
+            dst = tile(name, [P, PACK, P], dtype)
+            copy(dst[:].rearrange("p t m -> p m t"), src[:].rearrange("p (m t) -> p m t", t=PACK))
+            return dst
+
+        def gather(name, table, index, dtype):
+            dst = tile(name, [P, 16 * index.shape[1]], dtype)
+            nc.vector.tensor_copy(dst[:], table[:].indirect(index[:]))
+            return dst
+
+        def load_factor(name, src):
+            dst = tile(name, [P, PACK], F32)
+            nc.sync.dma_start(dst[:], src.rearrange("(p t) one -> p (t one)", t=PACK))
+            return dst
+
+        xt_plane = zeroed_plane("xt_plane", T)
+        xo_plane = zeroed_plane("xo_plane", Z)
+        w_plane = zeroed_plane("w_plane", R)
+        w2_plane = zeroed_plane("w2_plane", R)
+        ws_plane = zeroed_plane("ws_plane", N)
+        wb_plane = zeroed_plane("wb_plane", N)
+        pages = [tile(f"page{h}", [P, E], F32) for h in range(N // P)]
+        for page in pages:
+            nc.vector.memset(page[:], 0.0)
+
+        idx = load_list("idx", offs)
+        xt_staged = load_staged("xt_staged", xt_scales, T, nc.sync)
+        w_staged = load_staged("w_staged", w_scales, R, nc.sync)
+        w2_staged = load_staged("w2_staged", w2_scales, R, nc.sync)
+        w_raw = load_words("w_raw", w_words, R, U16, nc.sync)
+        xt = load_words("xt", xt_words, T, U32, nc.sync)
+        w2_raw = load_words("w2_raw", w2_words, R, U32, nc.sync)
+        xo = load_words("xo", xo_words, Z, U16, nc.sync)
+        load_plane(xo_plane, xo_scales, nc.sync)
+        idx2 = load_list("idx2", offs2)
+        idx3 = load_list("idx3", offs3)
+        sa_cols = load_factor("sa_cols", sa)
+        idx4 = load_list("idx4", offs4)
+        sg_cols = load_factor("sg_cols", sg)
+        idx5 = load_list("idx5", offs5)
+        sb_cols = load_factor("sb_cols", sb)
+        idx6 = load_list("idx6", offs6)
+        ws = load_words("ws", ws_words, N, U32, nc.sync)
+        load_plane(ws_plane, ws_scales, nc.sync)
+        wb = load_words("wb", wb_words, N, U32, nc.sync)
+        load_plane(wb_plane, wb_scales, nc.sync)
+        idx7 = load_list("idx7", offs7)
+
+        spread(xt_plane, xt_staged)
+        spread(w_plane, w_staged)
+        spread(w2_plane, w2_staged)
+        xt_picked_plane = gather("xt_picked_plane", xt_plane, idx, U8)
+        w_dealt_plane = deal(nc.vector.tensor_copy, "w_dealt_plane", w_plane, U8)
+        w_dealt = deal(nc.scalar.copy, "w_dealt", w_raw, U16)
+        xt_picked = gather("xt_picked", xt, idx, U32)
+        a_rows = []
+        for t in range(PACK):
+            bank = psum.tile([P, J], F32, name=f"a_bank{t}")
+            nc.tensor.matmul_mx(
+                out=bank[:], lhsT=w_dealt[:, t, :].bitcast(E2M1), lhsT_scale=w_dealt_plane[:, t, :],
+                rhs=xt_picked[:].bitcast(E4M3), rhs_scale=xt_picked_plane[:], start=True, stop=True,
+            )
+            rows = tile(f"a_rows{t}", [P, J], F32)
+            nc.scalar.copy(rows[:], bank[:])
+            a_rows.append(rows)
+
+        w2_dealt_plane = deal(nc.vector.tensor_copy, "w2_dealt_plane", w2_plane, U8)
+        w2_dealt = deal(nc.scalar.copy, "w2_dealt", w2_raw, U32)
+        xo_picked_plane = gather("xo_picked_plane", xo_plane, idx2, U8)
+        xo_picked = gather("xo_picked", xo, idx2, U16)
+        b_rows = []
+        for t in range(PACK):
+            bank = psum.tile([P, J], F32, name=f"b_bank{t}")
+            nc.tensor.matmul_mx(
+                out=bank[:], lhsT=w2_dealt[:, t, :].bitcast(E5M2), lhsT_scale=w2_dealt_plane[:, t, :],
+                rhs=xo_picked[:].bitcast(E2M1), rhs_scale=xo_picked_plane[:], start=True, stop=True,
+            )
+            rows = tile(f"b_rows{t}", [P, J], F32)
+            nc.vector.tensor_copy(rows[:], bank[:])
+            b_rows.append(rows)
+
+        a_scaled = tile("a_scaled", [P, PACK, O], F32)
+        for t in range(PACK):
+            nc.scalar.activation(a_scaled[:, t, :], a_rows[t][:].indirect(idx3[:]), ACT.Copy, scale=sa_cols[:, t : t + 1])
+        gate = tile("gate", [P, PACK, O], F32)
+        gated = tile("gated", [P, PACK, O], F32)
+        for t in range(PACK):
+            nc.scalar.activation(
+                gate[:, t, :], a_rows[t][:].indirect(idx4[:]), ACT.Sigmoid,
+                bias=b_rows[t][:, 0:1], scale=sg_cols[:, t : t + 1],
+            )
+            nc.vector.tensor_tensor(gated[:, t, :], a_scaled[:, t, :], gate[:, t, :], ALU.mult)
+
+        short_plane = gather("short_plane", xt_plane, idx6, U8)
+        short = gather("short", xt, idx6, U32)
+        p_banks = []
+        for h in range(N // P):
+            cols = slice(h * P, (h + 1) * P)
+            bank = psum.tile([P, O], F32, name=f"p_bank{h}", tag=f"a_bank{h}")
+            nc.tensor.matmul_mx(
+                out=bank[:], lhsT=ws[:, cols].bitcast(E5M2), lhsT_scale=ws_plane[:, cols],
+                rhs=short[:].bitcast(E4M3), rhs_scale=short_plane[:], start=True, stop=False,
+            )
+            p_banks.append(bank)
+
+        b_scaled = tile("b_scaled", [P, PACK, O], F32)
+        hid = tile("hid", [P, PACK, O], BF16)
+        for t in range(PACK):
+            nc.scalar.activation(b_scaled[:, t, :], b_rows[t][:].indirect(idx5[:]), ACT.Copy, scale=sb_cols[:, t : t + 1])
+            nc.vector.tensor_tensor(hid[:, t, :], gated[:, t, :], b_scaled[:, t, :], ALU.subtract)
+
+        woven = tile("woven", [P, O, PACK], BF16)
+        nc.vector.tensor_copy(
+            woven[:].rearrange("p (c i) t -> p c t i", i=4), hid[:].rearrange("p t (c i) -> p c t i", i=4)
+        )
+        hid_words = tile("hid_words", [P, O], U32)
+        hid_plane = tile("hid_plane", [P, O], U8)
+        nc.vector.quantize_mx(
+            out=hid_words[:].bitcast(E4M3), scales=hid_plane[:], in_=woven[:].rearrange("p o t -> p (o t)")
+        )
+
+        for h in range(N // P):
+            cols = slice(h * P, (h + 1) * P)
+            nc.tensor.matmul_mx(
+                out=p_banks[h][:], lhsT=wb[:, cols].bitcast(E5M2), lhsT_scale=wb_plane[:, cols],
+                rhs=hid_words[:].bitcast(E4M3), rhs_scale=hid_plane[:], start=False, stop=True,
+            )
+        p_rows = [tile(f"p_rows{h}", [P, O], F32) for h in range(N // P)]
+        nc.vector.tensor_copy(p_rows[0][:], p_banks[0][:])
+        nc.vector.tensor_copy(pages[0][:].indirect(idx7[:]), p_rows[0][:])
+        nc.sync.dma_start(out[0:P, :], pages[0][:])
+        nc.scalar.copy(p_rows[1][:], p_banks[1][:])
+        nc.scalar.activation(pages[1][:].indirect(idx7[:]), p_rows[1][:], ACT.Copy)
+        nc.scalar.dma_start(out[P:N, :], pages[1][:])

@@ -56,18 +56,20 @@ def tile_list_offsetlead_twotab_further_scattered_kernel(
             for q in range(QUADS):
                 queue.dma_start(plane[32 * q : 32 * q + ROWS, :].bitcast(I32), src[0, ROWS * q : ROWS * (q + 1), :].bitcast(I32))
 
-        def load_staged(name, src, columns, queue):
-            dst = tile(name, [ROWS, QUADS, columns // 4], I32)
-            queue.dma_start(dst[:], src[0].bitcast(I32).rearrange("(q r) c -> r q c", r=ROWS))
-            return dst
+        def stage(name, partitions, columns):
+            return tile(name, [partitions, 2, columns // 4], I32)
 
-        def spread(plane, staged):
-            for q in range(QUADS):
-                nc.vector.tensor_copy(plane[32 * q : 32 * q + ROWS, :].bitcast(I32), staged[:, q, :])
+        def load_stage(dst, src):
+            rows = src[0].bitcast(I32).rearrange("(u q r) c -> q r u c", u=2, r=ROWS)
+            for q in range(2):
+                nc.sync.dma_start(dst[32 * q : 32 * q + ROWS], rows[q])
 
         def deal(copy, name, src, dtype):
             dst = tile(name, [P, PACK, P], dtype)
-            copy(dst[:].rearrange("p t m -> p m t"), src[:].rearrange("p (m t) -> p m t", t=PACK))
+            if dtype == U32:
+                copy(dst[:].rearrange("p t m -> p m t"), src.rearrange("p (m t) -> p m t", t=PACK))
+            else:
+                copy(dst[:], src.rearrange("p (m t) -> p t m", t=PACK))
             return dst
 
         def gather(name, table, index, dtype):
@@ -80,45 +82,52 @@ def tile_list_offsetlead_twotab_further_scattered_kernel(
             nc.sync.dma_start(dst[:], src.rearrange("(p t) one -> p (t one)", t=PACK))
             return dst
 
-        xt_plane = zeroed_plane("xt_plane", T)
-        xo_plane = zeroed_plane("xo_plane", Z)
-        w_plane = zeroed_plane("w_plane", R)
-        w2_plane = zeroed_plane("w2_plane", R)
+        xt_stage = stage("xt_stage", 64, T)
+        w_stage = stage("w_stage", P, R)
+        xo_stage = stage("xo_stage", 64, Z)
+        w2_stage = stage("w2_stage", P, R)
+        nc.vector.memset(xt_stage[:, 0, :], 0)
+        nc.gpsimd.memset(xt_stage[:, 1, :], 0)
+        nc.vector.memset(w_stage[:], 0)
+        nc.gpsimd.memset(xo_stage[:], 0)
+        nc.vector.memset(w2_stage[:], 0)
         ws_plane = zeroed_plane("ws_plane", N)
         wb_plane = zeroed_plane("wb_plane", N)
         pages = [tile(f"page{h}", [P, E], F32) for h in range(N // P)]
-        for page in pages:
-            nc.vector.memset(page[:], 0.0)
+        nc.gpsimd.memset(pages[0][:], 0.0)
+        nc.vector.memset(pages[1][:], 0.0)
 
         idx = load_list("idx", offs)
-        xt_staged = load_staged("xt_staged", xt_scales, T, nc.sync)
-        w_staged = load_staged("w_staged", w_scales, R, nc.sync)
-        w2_staged = load_staged("w2_staged", w2_scales, R, nc.sync)
+        idx2 = load_list("idx2", offs2)
         w_raw = load_words("w_raw", w_words, R, U16, nc.sync)
+        load_stage(xt_stage, xt_scales)
+        load_stage(w_stage, w_scales)
         xt = load_words("xt", xt_words, T, U32, nc.sync)
         w2_raw = load_words("w2_raw", w2_words, R, U32, nc.sync)
         xo = load_words("xo", xo_words, Z, U16, nc.sync)
-        load_plane(xo_plane, xo_scales, nc.sync)
-        idx2 = load_list("idx2", offs2)
+        load_stage(xo_stage, xo_scales)
+        load_stage(w2_stage, w2_scales)
         idx3 = load_list("idx3", offs3)
         sa_cols = load_factor("sa_cols", sa)
         idx4 = load_list("idx4", offs4)
         sg_cols = load_factor("sg_cols", sg)
         idx5 = load_list("idx5", offs5)
         sb_cols = load_factor("sb_cols", sb)
-        idx6 = load_list("idx6", offs6)
         ws = load_words("ws", ws_words, N, U32, nc.sync)
-        load_plane(ws_plane, ws_scales, nc.sync)
         wb = load_words("wb", wb_words, N, U32, nc.sync)
-        load_plane(wb_plane, wb_scales, nc.sync)
+        idx6 = load_list("idx6", offs6)
         idx7 = load_list("idx7", offs7)
+        load_plane(ws_plane, ws_scales, nc.sync)
+        load_plane(wb_plane, wb_scales, nc.sync)
 
-        spread(xt_plane, xt_staged)
-        spread(w_plane, w_staged)
-        spread(w2_plane, w2_staged)
+        xt_plane = tile("xt_plane", [P, T], U8)
+        nc.vector.tensor_copy(xt_plane[0:64, :].bitcast(I32), xt_stage[:, 0, :])
+        nc.vector.tensor_copy(xt_plane[64:P, :].bitcast(I32), xt_stage[:, 1, :])
+        nc.vector.tensor_copy(w_stage[64:P, 0, :], w_stage[0:64, 1, :])
         xt_picked_plane = gather("xt_picked_plane", xt_plane, idx, U8)
-        w_dealt_plane = deal(nc.vector.tensor_copy, "w_dealt_plane", w_plane, U8)
-        w_dealt = deal(nc.scalar.copy, "w_dealt", w_raw, U16)
+        w_dealt_plane = deal(nc.vector.tensor_copy, "w_dealt_plane", w_stage[:, 0, :].bitcast(U8), U8)
+        w_dealt = deal(nc.scalar.copy, "w_dealt", w_raw[:], U16)
+        w2_dealt = deal(nc.scalar.copy, "w2_dealt", w2_raw[:], U32)
         xt_picked = gather("xt_picked", xt, idx, U32)
         a_rows = []
         for t in range(PACK):
@@ -131,10 +140,13 @@ def tile_list_offsetlead_twotab_further_scattered_kernel(
             nc.scalar.copy(rows[:], bank[:])
             a_rows.append(rows)
 
-        w2_dealt_plane = deal(nc.vector.tensor_copy, "w2_dealt_plane", w2_plane, U8)
-        w2_dealt = deal(nc.scalar.copy, "w2_dealt", w2_raw, U32)
-        xo_picked_plane = gather("xo_picked_plane", xo_plane, idx2, U8)
         xo_picked = gather("xo_picked", xo, idx2, U16)
+        xo_plane = tile("xo_plane", [P, Z], U8)
+        nc.vector.tensor_copy(xo_plane[0:64, :].bitcast(I32), xo_stage[:, 0, :])
+        nc.vector.tensor_copy(xo_plane[64:P, :].bitcast(I32), xo_stage[:, 1, :])
+        nc.vector.tensor_copy(w2_stage[64:P, 0, :], w2_stage[0:64, 1, :])
+        xo_picked_plane = gather("xo_picked_plane", xo_plane, idx2, U8)
+        w2_dealt_plane = deal(nc.vector.tensor_copy, "w2_dealt_plane", w2_stage[:, 0, :].bitcast(U8), U8)
         b_rows = []
         for t in range(PACK):
             bank = psum.tile([P, J], F32, name=f"b_bank{t}")

@@ -93,6 +93,9 @@ def tile_list_offsetlead_twotab_further_scattered_kernel(
         nc.vector.memset(w2_stage[:], 0)
         ws_plane = zeroed_plane("ws_plane", N)
         wb_plane = zeroed_plane("wb_plane", N)
+        warm = tile("warm", [P, 2], F32)
+        nc.vector.memset(warm[:, 0:1], 0.0)
+        nc.scalar.activation(warm[:, 1:2], warm[:, 0:1], ACT.Sigmoid)
         pages = [tile(f"page{h}", [P, E], F32) for h in range(N // P)]
         nc.gpsimd.memset(pages[0][:], 0.0)
         nc.vector.memset(pages[1][:], 0.0)

@@ -33,8 +33,8 @@ def tile_list_offsetlead_twotab_further_scattered_kernel(
         keep = ctx.enter_context(tc.tile_pool(name="keep", bufs=1))
         psum = ctx.enter_context(tc.psum_pool(name="psum", bufs=1))
 
-        def tile(name, shape, dtype):
-            return keep.tile(shape, dtype, name=name, align_bytes=64)
+        def tile(name, shape, dtype, tag=None):
+            return keep.tile(shape, dtype, name=name, tag=tag or name, align_bytes=64)
 
         def load_list(name, src):
             dst = lists.tile(list(src.shape), U16, name=name)
@@ -64,6 +64,9 @@ def tile_list_offsetlead_twotab_further_scattered_kernel(
             for q in range(2):
                 nc.sync.dma_start(dst[32 * q : 32 * q + ROWS], rows[q])
 
+        def load_rows(dst, src):
+            nc.sync.dma_start(dst, src[0].bitcast(I32).rearrange("(q r) c -> r q c", r=ROWS))
+
         def deal(copy, name, src, dtype):
             dst = tile(name, [P, PACK, P], dtype)
             if dtype == U32:
@@ -83,14 +86,11 @@ def tile_list_offsetlead_twotab_further_scattered_kernel(
             return dst
 
         xt_stage = stage("xt_stage", 64, T)
-        w_stage = stage("w_stage", P, R)
-        xo_stage = stage("xo_stage", 64, Z)
-        w2_stage = stage("w2_stage", P, R)
         nc.vector.memset(xt_stage[:, 0, :], 0)
         nc.gpsimd.memset(xt_stage[:, 1, :], 0)
-        nc.vector.memset(w_stage[:], 0)
-        nc.gpsimd.memset(xo_stage[:], 0)
-        nc.vector.memset(w2_stage[:], 0)
+        weight_stage = tile("weight_stage", [ROWS, QUADS, 2, R // 4], I32)
+        xo_plane = zeroed_plane("xo_plane", Z)
+        weight_plane = zeroed_plane("weight_plane", 2 * R)
         ws_plane = zeroed_plane("ws_plane", N)
         wb_plane = zeroed_plane("wb_plane", N)
         warm = tile("warm", [P, 2], F32)
@@ -100,16 +100,16 @@ def tile_list_offsetlead_twotab_further_scattered_kernel(
         nc.gpsimd.memset(pages[0][:], 0.0)
         nc.vector.memset(pages[1][:], 0.0)
 
+        load_rows(weight_stage[:, :, 0, :], w_scales)
+        load_rows(weight_stage[:, :, 1, :], w2_scales)
         idx = load_list("idx", offs)
-        idx2 = load_list("idx2", offs2)
         w_raw = load_words("w_raw", w_words, R, U16, nc.sync)
         load_stage(xt_stage, xt_scales)
-        load_stage(w_stage, w_scales)
         xt = load_words("xt", xt_words, T, U32, nc.sync)
         w2_raw = load_words("w2_raw", w2_words, R, U32, nc.sync)
         xo = load_words("xo", xo_words, Z, U16, nc.sync)
-        load_stage(xo_stage, xo_scales)
-        load_stage(w2_stage, w2_scales)
+        idx2 = load_list("idx2", offs2)
+        load_plane(xo_plane, xo_scales, nc.sync)
         idx3 = load_list("idx3", offs3)
         sa_cols = load_factor("sa_cols", sa)
         idx4 = load_list("idx4", offs4)
@@ -123,15 +123,21 @@ def tile_list_offsetlead_twotab_further_scattered_kernel(
         load_plane(ws_plane, ws_scales, nc.sync)
         load_plane(wb_plane, wb_scales, nc.sync)
 
+        for q in range(QUADS):
+            nc.vector.tensor_copy(
+                weight_plane[32 * q : 32 * q + ROWS, :].bitcast(I32), weight_stage[:, q].rearrange("p u c -> p (u c)")
+            )
         xt_plane = tile("xt_plane", [P, T], U8)
         nc.vector.tensor_copy(xt_plane[0:64, :].bitcast(I32), xt_stage[:, 0, :])
         nc.vector.tensor_copy(xt_plane[64:P, :].bitcast(I32), xt_stage[:, 1, :])
-        nc.vector.tensor_copy(w_stage[64:P, 0, :], w_stage[0:64, 1, :])
+        w_dealt_plane = deal(nc.vector.tensor_copy, "w_dealt_plane", weight_plane[:, 0:R], U8)
         xt_picked_plane = gather("xt_picked_plane", xt_plane, idx, U8)
-        w_dealt_plane = deal(nc.vector.tensor_copy, "w_dealt_plane", w_stage[:, 0, :].bitcast(U8), U8)
         w_dealt = deal(nc.scalar.copy, "w_dealt", w_raw[:], U16)
         w2_dealt = deal(nc.scalar.copy, "w2_dealt", w2_raw[:], U32)
         xt_picked = gather("xt_picked", xt, idx, U32)
+        xo_picked = gather("xo_picked", xo, idx2, U16)
+        w2_dealt_plane = deal(nc.vector.tensor_copy, "w2_dealt_plane", weight_plane[:, R : 2 * R], U8)
+        xo_picked_plane = gather("xo_picked_plane", xo_plane, idx2, U8)
         a_rows = []
         for t in range(PACK):
             bank = psum.tile([P, J], F32, name=f"a_bank{t}")
@@ -139,17 +145,10 @@ def tile_list_offsetlead_twotab_further_scattered_kernel(
                 out=bank[:], lhsT=w_dealt[:, t, :].bitcast(E2M1), lhsT_scale=w_dealt_plane[:, t, :],
                 rhs=xt_picked[:].bitcast(E4M3), rhs_scale=xt_picked_plane[:], start=True, stop=True,
             )
-            rows = tile(f"a_rows{t}", [P, J], F32)
-            nc.scalar.copy(rows[:], bank[:])
+            rows = tile(f"a_rows{t}", [P, J], F32, tag="xo_plane" if t == 3 else None)
+            (nc.scalar.copy if t < 3 else nc.vector.tensor_copy)(rows[:], bank[:])
             a_rows.append(rows)
 
-        xo_picked = gather("xo_picked", xo, idx2, U16)
-        xo_plane = tile("xo_plane", [P, Z], U8)
-        nc.vector.tensor_copy(xo_plane[0:64, :].bitcast(I32), xo_stage[:, 0, :])
-        nc.vector.tensor_copy(xo_plane[64:P, :].bitcast(I32), xo_stage[:, 1, :])
-        nc.vector.tensor_copy(w2_stage[64:P, 0, :], w2_stage[0:64, 1, :])
-        xo_picked_plane = gather("xo_picked_plane", xo_plane, idx2, U8)
-        w2_dealt_plane = deal(nc.vector.tensor_copy, "w2_dealt_plane", w2_stage[:, 0, :].bitcast(U8), U8)
         b_rows = []
         for t in range(PACK):
             bank = psum.tile([P, J], F32, name=f"b_bank{t}")
@@ -160,18 +159,6 @@ def tile_list_offsetlead_twotab_further_scattered_kernel(
             rows = tile(f"b_rows{t}", [P, J], F32)
             nc.vector.tensor_copy(rows[:], bank[:])
             b_rows.append(rows)
-
-        a_scaled = tile("a_scaled", [P, PACK, O], F32)
-        for t in range(PACK):
-            nc.scalar.activation(a_scaled[:, t, :], a_rows[t][:].indirect(idx3[:]), ACT.Copy, scale=sa_cols[:, t : t + 1])
-        gate = tile("gate", [P, PACK, O], F32)
-        gated = tile("gated", [P, PACK, O], F32)
-        for t in range(PACK):
-            nc.scalar.activation(
-                gate[:, t, :], a_rows[t][:].indirect(idx4[:]), ACT.Sigmoid,
-                bias=b_rows[t][:, 0:1], scale=sg_cols[:, t : t + 1],
-            )
-            nc.vector.tensor_tensor(gated[:, t, :], a_scaled[:, t, :], gate[:, t, :], ALU.mult)
 
         short_plane = gather("short_plane", xt_plane, idx6, U8)
         short = gather("short", xt, idx6, U32)
@@ -185,8 +172,20 @@ def tile_list_offsetlead_twotab_further_scattered_kernel(
             )
             p_banks.append(bank)
 
+        a_scaled = tile("a_scaled", [P, PACK, O], F32)
+        for t in range(PACK):
+            nc.scalar.activation(a_scaled[:, t, :], a_rows[t][:].indirect(idx3[:]), ACT.Copy, scale=sa_cols[:, t : t + 1])
+        gate = tile("gate", [P, PACK, O], F32)
+        gated = tile("gated", [P, PACK, O], F32, tag="xt")
+        for t in range(PACK):
+            nc.scalar.activation(
+                gate[:, t, :], a_rows[t][:].indirect(idx4[:]), ACT.Sigmoid,
+                bias=b_rows[t][:, 0:1], scale=sg_cols[:, t : t + 1],
+            )
+            nc.vector.tensor_tensor(gated[:, t, :], a_scaled[:, t, :], gate[:, t, :], ALU.mult)
+
         b_scaled = tile("b_scaled", [P, PACK, O], F32)
-        hid = tile("hid", [P, PACK, O], BF16)
+        hid = tile("hid", [P, PACK, O], BF16, tag="xt_plane")
         for t in range(PACK):
             nc.scalar.activation(b_scaled[:, t, :], b_rows[t][:].indirect(idx5[:]), ACT.Copy, scale=sb_cols[:, t : t + 1])
             nc.vector.tensor_tensor(hid[:, t, :], gated[:, t, :], b_scaled[:, t, :], ALU.subtract)

@@ -6,9 +6,15 @@ K, T, J, R, F, Z, O, N, E = 512, 1024, 256, 512, 512, 1024, 128, 256, 1024
 FLOPS = 2 * K * R * J + 2 * F * R * J + 2 * R * N * O + 2 * K * N * O
 
 P = 128
+HALF = P // 2
 PACK = 4
 QUADS = 4
+QUAD = P // QUADS
 ROWS = 4
+GROUP = 16
+I32_BYTES = 4
+LINE = 4
+A_BANKS_ON_SCALAR = 3
 
 F32 = mybir.dt.float32
 BF16 = mybir.dt.bfloat16
@@ -41,10 +47,15 @@ def tile_list_offsetlead_twotab_further_scattered_kernel(
             nc.sync.dma_start(dst[:], src)
             return dst
 
-        def load_words(name, src, columns, dtype, queue):
+        def load_words(name, src, columns, dtype):
             dst = tile(name, [P, columns], dtype)
-            rows = src[0] if src.ndim == 3 else src[0].rearrange("p c t -> p (c t)")
-            queue.dma_start(dst[:].bitcast(I32), rows.bitcast(I32))
+            byte_rows = src[0] if src.ndim == 3 else src[0].rearrange("p c t -> p (c t)")
+            nc.sync.dma_start(dst[:].bitcast(I32), byte_rows.bitcast(I32))
+            return dst
+
+        def load_factor(name, src):
+            dst = tile(name, [P, PACK], F32)
+            nc.sync.dma_start(dst[:], src.rearrange("(p t) one -> p (t one)", t=PACK))
             return dst
 
         def zeroed_plane(name, columns):
@@ -52,20 +63,11 @@ def tile_list_offsetlead_twotab_further_scattered_kernel(
             nc.vector.memset(dst[:].bitcast(I32), 0)
             return dst
 
-        def load_plane(plane, src, queue):
+        def load_plane(plane, src):
             for q in range(QUADS):
-                queue.dma_start(plane[32 * q : 32 * q + ROWS, :].bitcast(I32), src[0, ROWS * q : ROWS * (q + 1), :].bitcast(I32))
-
-        def stage(name, partitions, columns):
-            return tile(name, [partitions, 2, columns // 4], I32)
-
-        def load_stage(dst, src):
-            rows = src[0].bitcast(I32).rearrange("(u q r) c -> q r u c", u=2, r=ROWS)
-            for q in range(2):
-                nc.sync.dma_start(dst[32 * q : 32 * q + ROWS], rows[q])
-
-        def load_rows(dst, src):
-            nc.sync.dma_start(dst, src[0].bitcast(I32).rearrange("(q r) c -> r q c", r=ROWS))
+                nc.sync.dma_start(
+                    plane[QUAD * q : QUAD * q + ROWS, :].bitcast(I32), src[0, ROWS * q : ROWS * (q + 1), :].bitcast(I32)
+                )
 
         def deal(copy, name, src, dtype):
             dst = tile(name, [P, PACK, P], dtype)
@@ -76,19 +78,14 @@ def tile_list_offsetlead_twotab_further_scattered_kernel(
             return dst
 
         def gather(name, table, index, dtype):
-            dst = tile(name, [P, 16 * index.shape[1]], dtype)
+            dst = tile(name, [P, GROUP * index.shape[1]], dtype)
             nc.vector.tensor_copy(dst[:], table[:].indirect(index[:]))
             return dst
 
-        def load_factor(name, src):
-            dst = tile(name, [P, PACK], F32)
-            nc.sync.dma_start(dst[:], src.rearrange("(p t) one -> p (t one)", t=PACK))
-            return dst
-
-        xt_stage = stage("xt_stage", 64, T)
-        nc.vector.memset(xt_stage[:, 0, :], 0)
-        nc.gpsimd.memset(xt_stage[:, 1, :], 0)
-        weight_stage = tile("weight_stage", [ROWS, QUADS, 2, R // 4], I32)
+        xt_stage = tile("xt_stage", [P, 2, T // I32_BYTES], I32)
+        nc.vector.memset(xt_stage[HALF:P, 0, :], 0)
+        nc.gpsimd.memset(xt_stage[HALF:P, 1, :], 0)
+        weight_stage = tile("weight_stage", [ROWS, QUADS, 2, R // I32_BYTES], I32)
         xo_plane = zeroed_plane("xo_plane", Z)
         weight_plane = zeroed_plane("weight_plane", 2 * R)
         ws_plane = zeroed_plane("ws_plane", N)
@@ -97,39 +94,41 @@ def tile_list_offsetlead_twotab_further_scattered_kernel(
         nc.vector.memset(warm[:, 0:1], 0.0)
         nc.scalar.activation(warm[:, 1:2], warm[:, 0:1], ACT.Sigmoid)
         pages = [tile(f"page{h}", [P, E], F32) for h in range(N // P)]
-        nc.gpsimd.memset(pages[0][:], 0.0)
-        nc.vector.memset(pages[1][:], 0.0)
+        for page in pages:
+            nc.vector.memset(page[:], 0.0)
 
-        load_rows(weight_stage[:, :, 0, :], w_scales)
-        load_rows(weight_stage[:, :, 1, :], w2_scales)
+        for u, src in enumerate((w_scales, w2_scales)):
+            nc.sync.dma_start(weight_stage[:, :, u, :], src[0].bitcast(I32).rearrange("(q i) c -> i q c", i=ROWS))
         idx = load_list("idx", offs)
-        w_raw = load_words("w_raw", w_words, R, U16, nc.sync)
-        load_stage(xt_stage, xt_scales)
-        xt = load_words("xt", xt_words, T, U32, nc.sync)
-        w2_raw = load_words("w2_raw", w2_words, R, U32, nc.sync)
-        xo = load_words("xo", xo_words, Z, U16, nc.sync)
+        w_raw = load_words("w_raw", w_words, R, U16)
+        xt_blocks = xt_scales[0].bitcast(I32).rearrange("(u v i) c -> v i u c", u=2, i=ROWS)
+        for v in range(2):
+            nc.sync.dma_start(xt_stage[HALF + QUAD * v : HALF + QUAD * v + ROWS], xt_blocks[v])
+        xt = load_words("xt", xt_words, T, U32)
+        w2_raw = load_words("w2_raw", w2_words, R, U32)
+        xo = load_words("xo", xo_words, Z, U16)
         idx2 = load_list("idx2", offs2)
-        load_plane(xo_plane, xo_scales, nc.sync)
+        load_plane(xo_plane, xo_scales)
         idx3 = load_list("idx3", offs3)
         sa_cols = load_factor("sa_cols", sa)
         idx4 = load_list("idx4", offs4)
         sg_cols = load_factor("sg_cols", sg)
         idx5 = load_list("idx5", offs5)
         sb_cols = load_factor("sb_cols", sb)
-        ws = load_words("ws", ws_words, N, U32, nc.sync)
-        wb = load_words("wb", wb_words, N, U32, nc.sync)
+        ws = load_words("ws", ws_words, N, U32)
+        wb = load_words("wb", wb_words, N, U32)
         idx6 = load_list("idx6", offs6)
         idx7 = load_list("idx7", offs7)
-        load_plane(ws_plane, ws_scales, nc.sync)
-        load_plane(wb_plane, wb_scales, nc.sync)
+        load_plane(ws_plane, ws_scales)
+        load_plane(wb_plane, wb_scales)
 
         for q in range(QUADS):
             nc.vector.tensor_copy(
-                weight_plane[32 * q : 32 * q + ROWS, :].bitcast(I32), weight_stage[:, q].rearrange("p u c -> p (u c)")
+                weight_plane[QUAD * q : QUAD * q + ROWS, :].bitcast(I32), weight_stage[:, q].rearrange("p u c -> p (u c)")
             )
         xt_plane = tile("xt_plane", [P, T], U8)
-        nc.vector.tensor_copy(xt_plane[0:64, :].bitcast(I32), xt_stage[:, 0, :])
-        nc.vector.tensor_copy(xt_plane[64:P, :].bitcast(I32), xt_stage[:, 1, :])
+        for u in range(2):
+            nc.vector.tensor_copy(xt_plane[HALF * u : HALF * (u + 1), :].bitcast(I32), xt_stage[HALF:P, u, :])
         w_dealt_plane = deal(nc.vector.tensor_copy, "w_dealt_plane", weight_plane[:, 0:R], U8)
         xt_picked_plane = gather("xt_picked_plane", xt_plane, idx, U8)
         w_dealt = deal(nc.scalar.copy, "w_dealt", w_raw[:], U16)
@@ -138,6 +137,7 @@ def tile_list_offsetlead_twotab_further_scattered_kernel(
         xo_picked = gather("xo_picked", xo, idx2, U16)
         w2_dealt_plane = deal(nc.vector.tensor_copy, "w2_dealt_plane", weight_plane[:, R : 2 * R], U8)
         xo_picked_plane = gather("xo_picked_plane", xo_plane, idx2, U8)
+
         a_rows = []
         for t in range(PACK):
             bank = psum.tile([P, J], F32, name=f"a_bank{t}")
@@ -145,8 +145,12 @@ def tile_list_offsetlead_twotab_further_scattered_kernel(
                 out=bank[:], lhsT=w_dealt[:, t, :].bitcast(E2M1), lhsT_scale=w_dealt_plane[:, t, :],
                 rhs=xt_picked[:].bitcast(E4M3), rhs_scale=xt_picked_plane[:], start=True, stop=True,
             )
-            rows = tile(f"a_rows{t}", [P, J], F32, tag="xo_plane" if t == 3 else None)
-            (nc.scalar.copy if t < 3 else nc.vector.tensor_copy)(rows[:], bank[:])
+            if t < A_BANKS_ON_SCALAR:
+                rows = tile(f"a_rows{t}", [P, J], F32)
+                nc.scalar.copy(rows[:], bank[:])
+            else:
+                rows = tile(f"a_rows{t}", [P, J], F32, tag="xo_plane")
+                nc.vector.tensor_copy(rows[:], bank[:])
             a_rows.append(rows)
 
         b_rows = []
@@ -192,7 +196,7 @@ def tile_list_offsetlead_twotab_further_scattered_kernel(
 
         woven = tile("woven", [P, O, PACK], BF16)
         nc.vector.tensor_copy(
-            woven[:].rearrange("p (c i) t -> p c t i", i=4), hid[:].rearrange("p t (c i) -> p c t i", i=4)
+            woven[:].rearrange("p (c i) t -> p c t i", i=LINE), hid[:].rearrange("p t (c i) -> p c t i", i=LINE)
         )
         hid_words = tile("hid_words", [P, O], U32)
         hid_plane = tile("hid_plane", [P, O], U8)
@@ -206,6 +210,7 @@ def tile_list_offsetlead_twotab_further_scattered_kernel(
                 out=p_banks[h][:], lhsT=wb[:, cols].bitcast(E5M2), lhsT_scale=wb_plane[:, cols],
                 rhs=hid_words[:].bitcast(E4M3), rhs_scale=hid_plane[:], start=False, stop=True,
             )
+
         p_rows = [tile(f"p_rows{h}", [P, O], F32) for h in range(N // P)]
         nc.vector.tensor_copy(p_rows[0][:], p_banks[0][:])
         nc.vector.tensor_copy(pages[0][:].indirect(idx7[:]), p_rows[0][:])

from contextlib import ExitStack

import concourse.mybir as mybir

K, T, J, R, F, Z, O, N, E = 512, 1024, 256, 512, 512, 1024, 128, 256, 1024
FLOPS = 2 * K * R * J + 2 * F * R * J + 2 * R * N * O + 2 * K * N * O

P = 128
HALF = P // 2
PACK = 4
QUADS = 4
QUAD = P // QUADS
ROWS = 4
GROUP = 16
I32_BYTES = 4
LINE = 4
A_BANKS_ON_SCALAR = 3

F32 = mybir.dt.float32
BF16 = mybir.dt.bfloat16
I32 = mybir.dt.int32
U32 = mybir.dt.uint32
U16 = mybir.dt.uint16
U8 = mybir.dt.uint8
E4M3 = mybir.dt.float8_e4m3fn_x4
E5M2 = mybir.dt.float8_e5m2_x4
E2M1 = mybir.dt.float4_e2m1fn_x4
ACT = mybir.ActivationFunctionType
ALU = mybir.AluOpType


def tile_list_offsetlead_twotab_further_scattered_kernel(
    tc, xt_words, xt_scales, xo_words, xo_scales, w_words, w_scales, w2_words, w2_scales, sa, sb, sg,
    wb_words, wb_scales, ws_words, ws_scales, offs, offs2, offs3, offs4, offs5, offs6, offs7, out,
):
    nc = tc.nc
    with ExitStack() as ctx:
        lists = ctx.enter_context(tc.tile_pool(name="lists", bufs=1))
        keep = ctx.enter_context(tc.tile_pool(name="keep", bufs=1))
        psum = ctx.enter_context(tc.psum_pool(name="psum", bufs=1))

        def tile(name, shape, dtype, tag=None):
            return keep.tile(shape, dtype, name=name, tag=tag or name, align_bytes=64)

        def load_list(name, src):
            dst = lists.tile(list(src.shape), U16, name=name)
            nc.sync.dma_start(dst[:], src)
            return dst

        def load_words(name, src, columns, dtype):
            dst = tile(name, [P, columns], dtype)
            byte_rows = src[0] if src.ndim == 3 else src[0].rearrange("p c t -> p (c t)")
            nc.sync.dma_start(dst[:].bitcast(I32), byte_rows.bitcast(I32))
            return dst

        def load_factor(name, src):
            dst = tile(name, [P, PACK], F32)
            nc.sync.dma_start(dst[:], src.rearrange("(p t) one -> p (t one)", t=PACK))
            return dst

        def zeroed_plane(name, columns):
            dst = tile(name, [P, columns], U8)
            nc.vector.memset(dst[:].bitcast(I32), 0)
            return dst

        def load_plane(plane, src):
            for q in range(QUADS):
                nc.sync.dma_start(
                    plane[QUAD * q : QUAD * q + ROWS, :].bitcast(I32), src[0, ROWS * q : ROWS * (q + 1), :].bitcast(I32)
                )

        def deal(copy, name, src, dtype):
            dst = tile(name, [P, PACK, P], dtype)
            if dtype == U32:
                copy(dst[:].rearrange("p t m -> p m t"), src.rearrange("p (m t) -> p m t", t=PACK))
            else:
                copy(dst[:], src.rearrange("p (m t) -> p t m", t=PACK))
            return dst

        def gather(name, table, index, dtype):
            dst = tile(name, [P, GROUP * index.shape[1]], dtype)
            nc.vector.tensor_copy(dst[:], table[:].indirect(index[:]))
            return dst

        xt_stage = tile("xt_stage", [P, 2, T // I32_BYTES], I32)
        nc.vector.memset(xt_stage[HALF:P, 0, :], 0)
        nc.gpsimd.memset(xt_stage[HALF:P, 1, :], 0)
        weight_stage = tile("weight_stage", [ROWS, QUADS, 2, R // I32_BYTES], I32)
        xo_plane = zeroed_plane("xo_plane", Z)
        weight_plane = zeroed_plane("weight_plane", 2 * R)
        ws_plane = zeroed_plane("ws_plane", N)
        wb_plane = zeroed_plane("wb_plane", N)
        warm = tile("warm", [P, 2], F32)
        nc.vector.memset(warm[:, 0:1], 0.0)
        nc.scalar.activation(warm[:, 1:2], warm[:, 0:1], ACT.Sigmoid)
        pages = [tile(f"page{h}", [P, E], F32) for h in range(N // P)]
        for page in pages:
            nc.vector.memset(page[:], 0.0)

        for u, src in enumerate((w_scales, w2_scales)):
            nc.sync.dma_start(weight_stage[:, :, u, :], src[0].bitcast(I32).rearrange("(q i) c -> i q c", i=ROWS))
        idx = load_list("idx", offs)
        w_raw = load_words("w_raw", w_words, R, U16)
        xt_blocks = xt_scales[0].bitcast(I32).rearrange("(u v i) c -> v i u c", u=2, i=ROWS)
        for v in range(2):
            nc.sync.dma_start(xt_stage[HALF + QUAD * v : HALF + QUAD * v + ROWS], xt_blocks[v])
        xt = load_words("xt", xt_words, T, U32)
        w2_raw = load_words("w2_raw", w2_words, R, U32)
        xo = load_words("xo", xo_words, Z, U16)
        idx2 = load_list("idx2", offs2)
        load_plane(xo_plane, xo_scales)
        idx3 = load_list("idx3", offs3)
        sa_cols = load_factor("sa_cols", sa)
        idx4 = load_list("idx4", offs4)
        sg_cols = load_factor("sg_cols", sg)
        idx5 = load_list("idx5", offs5)
        sb_cols = load_factor("sb_cols", sb)
        ws = load_words("ws", ws_words, N, U32)
        wb = load_words("wb", wb_words, N, U32)
        idx6 = load_list("idx6", offs6)
        idx7 = load_list("idx7", offs7)
        load_plane(ws_plane, ws_scales)
        load_plane(wb_plane, wb_scales)

        for q in range(QUADS):
            nc.vector.tensor_copy(
                weight_plane[QUAD * q : QUAD * q + ROWS, :].bitcast(I32), weight_stage[:, q].rearrange("p u c -> p (u c)")
            )
        xt_plane = tile("xt_plane", [P, T], U8)
        for u in range(2):
            nc.vector.tensor_copy(xt_plane[HALF * u : HALF * (u + 1), :].bitcast(I32), xt_stage[HALF:P, u, :])
        w_dealt_plane = deal(nc.vector.tensor_copy, "w_dealt_plane", weight_plane[:, 0:R], U8)
        xt_picked_plane = gather("xt_picked_plane", xt_plane, idx, U8)
        w_dealt = deal(nc.scalar.copy, "w_dealt", w_raw[:], U16)
        w2_dealt = deal(nc.scalar.copy, "w2_dealt", w2_raw[:], U32)
        xt_picked = gather("xt_picked", xt, idx, U32)
        xo_picked = gather("xo_picked", xo, idx2, U16)
        w2_dealt_plane = deal(nc.vector.tensor_copy, "w2_dealt_plane", weight_plane[:, R : 2 * R], U8)
        xo_picked_plane = gather("xo_picked_plane", xo_plane, idx2, U8)

        a_rows = []
        for t in range(PACK):
            bank = psum.tile([P, J], F32, name=f"a_bank{t}")
            nc.tensor.matmul_mx(
                out=bank[:], lhsT=w_dealt[:, t, :].bitcast(E2M1), lhsT_scale=w_dealt_plane[:, t, :],
                rhs=xt_picked[:].bitcast(E4M3), rhs_scale=xt_picked_plane[:], start=True, stop=True,
            )
            if t < A_BANKS_ON_SCALAR:
                rows = tile(f"a_rows{t}", [P, J], F32)
                nc.scalar.copy(rows[:], bank[:])
            else:
                rows = tile(f"a_rows{t}", [P, J], F32, tag="xo_plane")
                nc.vector.tensor_copy(rows[:], bank[:])
            a_rows.append(rows)

        b_rows = []
        for t in range(PACK):
            bank = psum.tile([P, J], F32, name=f"b_bank{t}")
            nc.tensor.matmul_mx(
                out=bank[:], lhsT=w2_dealt[:, t, :].bitcast(E5M2), lhsT_scale=w2_dealt_plane[:, t, :],
                rhs=xo_picked[:].bitcast(E2M1), rhs_scale=xo_picked_plane[:], start=True, stop=True,
            )
            rows = tile(f"b_rows{t}", [P, J], F32)
            nc.vector.tensor_copy(rows[:], bank[:])
            b_rows.append(rows)

        short_plane = gather("short_plane", xt_plane, idx6, U8)
        short = gather("short", xt, idx6, U32)
        p_banks = []
        for h in range(N // P):
            cols = slice(h * P, (h + 1) * P)
            bank = psum.tile([P, O], F32, name=f"p_bank{h}", tag=f"a_bank{h}")
            nc.tensor.matmul_mx(
                out=bank[:], lhsT=ws[:, cols].bitcast(E5M2), lhsT_scale=ws_plane[:, cols],
                rhs=short[:].bitcast(E4M3), rhs_scale=short_plane[:], start=True, stop=False,
            )
            p_banks.append(bank)

        a_scaled = tile("a_scaled", [P, PACK, O], F32)
        for t in range(PACK):
            nc.scalar.activation(a_scaled[:, t, :], a_rows[t][:].indirect(idx3[:]), ACT.Copy, scale=sa_cols[:, t : t + 1])
        gate = tile("gate", [P, PACK, O], F32)
        gated = tile("gated", [P, PACK, O], F32, tag="xt")
        for t in range(PACK):
            nc.scalar.activation(
                gate[:, t, :], a_rows[t][:].indirect(idx4[:]), ACT.Sigmoid,
                bias=b_rows[t][:, 0:1], scale=sg_cols[:, t : t + 1],
            )
            nc.vector.tensor_tensor(gated[:, t, :], a_scaled[:, t, :], gate[:, t, :], ALU.mult)

        b_scaled = tile("b_scaled", [P, PACK, O], F32)
        hid = tile("hid", [P, PACK, O], BF16, tag="xt_plane")
        for t in range(PACK):
            nc.scalar.activation(b_scaled[:, t, :], b_rows[t][:].indirect(idx5[:]), ACT.Copy, scale=sb_cols[:, t : t + 1])
            nc.vector.tensor_tensor(hid[:, t, :], gated[:, t, :], b_scaled[:, t, :], ALU.subtract)

        woven = tile("woven", [P, O, PACK], BF16)
        nc.vector.tensor_copy(
            woven[:].rearrange("p (c i) t -> p c t i", i=LINE), hid[:].rearrange("p t (c i) -> p c t i", i=LINE)
        )
        hid_words = tile("hid_words", [P, O], U32)
        hid_plane = tile("hid_plane", [P, O], U8)
        nc.vector.quantize_mx(
            out=hid_words[:].bitcast(E4M3), scales=hid_plane[:], in_=woven[:].rearrange("p o t -> p (o t)")
        )

        for h in range(N // P):
            cols = slice(h * P, (h + 1) * P)
            nc.tensor.matmul_mx(
                out=p_banks[h][:], lhsT=wb[:, cols].bitcast(E5M2), lhsT_scale=wb_plane[:, cols],
                rhs=hid_words[:].bitcast(E4M3), rhs_scale=hid_plane[:], start=False, stop=True,
            )

        p_rows = [tile(f"p_rows{h}", [P, O], F32) for h in range(N // P)]
        nc.vector.tensor_copy(p_rows[0][:], p_banks[0][:])
        nc.vector.tensor_copy(pages[0][:].indirect(idx7[:]), p_rows[0][:])
        nc.sync.dma_start(out[0:P, :], pages[0][:])
        nc.scalar.copy(p_rows[1][:], p_banks[1][:])
        nc.scalar.activation(pages[1][:].indirect(idx7[:]), p_rows[1][:], ACT.Copy)
        nc.scalar.dma_start(out[P:N, :], pages[1][:])
